import numpy as np
import ml_dtypes


def mxq(x, axis, fmt="e4m3"):
    dtype, down = {"e4m3": (ml_dtypes.float8_e4m3fn, 7), "e5m2": (ml_dtypes.float8_e5m2, 14)}[fmt]
    v = np.moveaxis(np.asarray(x, np.float32).astype(ml_dtypes.bfloat16).astype(np.float64), axis, -1)
    blocks = v.reshape(v.shape[:-1] + (-1, 32))
    amax = np.abs(blocks).max(-1, keepdims=True)
    byte = np.maximum(np.where(amax > 0, np.frexp(amax)[1] - 1 + 127, 0) - down, 1)
    scale = np.exp2(byte - 127.0)
    codes = (blocks / scale).astype(np.float32).astype(dtype).astype(np.float64)
    return np.moveaxis((codes * scale).reshape(v.shape), -1, axis)


WIDE = False


def mx_kscale(k):
    if not WIDE:
        return np.ones(k)
    levels = np.array([10, -10, 5, -5, 0])
    if k % 512:
        return np.exp2(np.random.permutation(np.resize(levels, k // 32))).repeat(32)
    a = np.empty((k // 512, 16))
    for p in range(k // 512):
        a[p, :8] = np.random.permutation(np.resize(levels, 8))
        for g in range(8):
            far = levels[np.abs(levels - a[p, g]) >= 10]
            a[p, g + 8] = far[np.random.randint(len(far))]
    return np.exp2(a.ravel()).repeat(32)


def f64(x):
    return np.asarray(x).astype(np.float64)


def striped(idx):
    return np.tile(idx.reshape(-1, 16).T, (8, 1)).astype(np.uint16)


def unstriped(offs):
    return offs[:16].T.reshape(-1).astype(np.int64)


def pack_weight(w):
    k, n = w.shape
    w = f64(np.asarray(w, np.float32).astype(ml_dtypes.bfloat16)).reshape(k // 32, 32, n)
    amax = np.abs(w).max(1)
    byte = np.clip(np.where(amax > 0, np.frexp(amax)[1] - 1 + 127 - 7, 1), 1, 254)
    scaled = (w * np.exp2(127.0 - byte)[:, None, :]).reshape(k, n).astype(np.float32)
    words = np.ascontiguousarray(scaled.reshape(k // 512, 128, 4, n).transpose(0, 1, 3, 2)).astype(ml_dtypes.float8_e4m3fn).view(np.uint8)
    return words, np.ascontiguousarray(byte.astype(np.uint8).reshape(k // 512, 16, n))


def unpack_weight(words, scales):
    g, p, n, _ = words.shape
    vals = np.ascontiguousarray(words).view(ml_dtypes.float8_e4m3fn).astype(np.float64) * np.repeat(np.exp2(scales.astype(np.float64) - 127.0), 8, axis=1)[..., None]
    return vals.transpose(0, 1, 3, 2).reshape(g * 512, n)


def silu(v):
    return v / (1.0 + np.exp(-np.maximum(v, -700.0)))


K, T, S, D, N, H = 512, 2048, 512, 4, 256, 512
P = 2 ** 7


def setup_inputs():
    n = np.random.standard_normal
    s = mx_kscale(K)[:, None]
    u = mx_kscale(H)
    packed_xT = pack_weight(n((K, T)) * s)
    return {
        "x_words": packed_xT[0],
        "x_scales": packed_xT[1],
        "w1": (n((K, H)) / np.sqrt(K) / s).astype(np.float32),
        "wg": (n((K, H)) / np.sqrt(K) / s).astype(np.float32),
        "stat": (np.tile(np.random.uniform(0.1, 0.5, S), (P, 1))).astype(np.float32),
        "unit": (np.random.uniform(0.5, 1.5, (H, 1)) * u[:, None]).astype(np.float32),
        "wo": (n((H, N)) / np.sqrt(H) / u[:, None]).astype(np.float32),
        "offs": striped(np.random.permutation(T)[:S]),
    }


def reference(x_words, x_scales, w1, wg, stat, unit, wo, offs):
    xq = unpack_weight(x_words, x_scales)[:, unstriped(offs)]
    gt = np.tanh(mxq(f64(wg), 0, "e4m3").T @ xq)
    al = gt * (0.5 * f64(stat)[:1]) + f64(stat)[:1]
    hs = mxq(f64(w1), 0, "e4m3").T @ xq
    ah = al * hs
    inp = ah.reshape(len(ah), -1, D).sum(axis=2)
    mid = silu(inp)
    zz = f64(unit) * mid
    return mxq(f64(wo), 0, "e4m3").T @ mxq(zz, 0, "e4m3")

@@ -1,0 +1,217 @@
+from contextlib import ExitStack
+
+import concourse.mybir as mybir
+from concourse.masks import make_identity
+
+K, T, S, D, N, H = 512, 2048, 512, 4, 256, 512
+V = S // D
+P = 128
+PACK = 4
+HALF = H // 2
+FLOPS = 2 * (2 * K * H * S + H * N * V)
+
+F32 = mybir.dt.float32
+BF16 = mybir.dt.bfloat16
+I32 = mybir.dt.int32
+U32 = mybir.dt.uint32
+U16 = mybir.dt.uint16
+U8 = mybir.dt.uint8
+FP8X4 = mybir.dt.float8_e4m3fn_x4
+ACT = mybir.ActivationFunctionType
+ALU = mybir.AluOpType
+
+
+def tile_picked_yhyper_in_p_kernel(
+    tc, x_words, x_scales, w1, wg, stat, unit, wo, offs, out
+):
+    nc = tc.nc
+    with ExitStack() as ctx:
+        sb = ctx.enter_context(tc.tile_pool(name="sb", bufs=1))
+        ps = ctx.enter_context(tc.psum_pool(name="ps", bufs=1))
+
+        def load(name, w, c0, width):
+            raw = sb.tile([P, PACK, width], F32, name=name)
+            nc.sync.dma_start(raw[:], w.rearrange("(p j) c -> p j c", j=PACK)[:, :, c0 : c0 + width])
+            return raw
+
+        scale_table = sb.tile([P, T], U8, name="scale_table")
+        nc.vector.memset(scale_table[:].bitcast(I32), 0)
+
+        offsets = sb.tile([P, S // 16], U16, name="offsets")
+        nc.sync.dma_start(offsets[:], offs)
+        raw_ga = load("raw_ga", wg, 0, HALF)
+        for q in range(4):
+            nc.sync.dma_start(
+                scale_table[32 * q : 32 * q + 4, :].bitcast(I32),
+                x_scales[0, 4 * q : 4 * q + 4, :].bitcast(I32),
+            )
+        x_table = sb.tile([P, T], I32, name="x_table")
+        nc.sync.dma_start(x_table[:], x_words[0].rearrange("p n t -> p (n t)").bitcast(I32))
+        raw_gb = load("raw_gb", wg, HALF, HALF)
+        raw_1a = load("raw_1a", w1, 0, 256)
+        raw_1b = load("raw_1b", w1, 256, 128)
+        raw_1c = load("raw_1c", w1, 384, 128)
+        raw_o = load("raw_o", wo, 0, N)
+
+        stat_vd = sb.tile([P, D], F32, name="stat_vd")
+        nc.gpsimd.dma_start(stat_vd[:], stat[0, :].rearrange("(v d) -> v d", d=D))
+        unit_pt = sb.tile([P, PACK], F32, name="unit_pt")
+        nc.gpsimd.dma_start(unit_pt[:], unit.rearrange("(p t) o -> p (t o)", t=PACK))
+        stat2_vd = sb.tile([P, D], F32, name="stat2_vd")
+        nc.gpsimd.tensor_scalar(stat2_vd[:], stat_vd[:], 2.0, 0.0, ALU.mult, ALU.add)
+        ident = sb.tile([P, P], F32, name="ident")
+        make_identity(nc, ident[:])
+
+        def grouped_tile(name, width):
+            return sb.tile([P, width, PACK], BF16, name=name, align_bytes=64)
+
+        def cast(copy, dst, raw, c0, c1):
+            copy(
+                dst[:, c0:c1, :].rearrange("p (c i) t -> p c t i", i=4),
+                raw[:, :, c0:c1].rearrange("p t (c i) -> p c t i", i=4),
+            )
+
+        def quantize(name, grouped, width):
+            codes = sb.tile([P, width], U32, name=name + "_codes", align_bytes=64)
+            scales = sb.tile([P, width], U8, name=name + "_scales", align_bytes=64)
+            nc.vector.quantize_mx(
+                out=codes[:].bitcast(FP8X4), scales=scales[:], in_=grouped[:].rearrange("p c t -> p (c t)")
+            )
+            return codes, scales
+
+        def project(name, tags, w, width):
+            codes, scales = w
+            per_bank = 512 // width
+            banks = []
+            for e in range(D // per_bank):
+                bank = ps.tile([P, per_bank, width], F32, name=name + str(e), tag=tags[e])
+                for dd in range(per_bank):
+                    d = per_bank * e + dd
+                    nc.tensor.matmul_mx(
+                        out=bank[:, dd, :],
+                        lhsT=x_codes[:, d, :].bitcast(FP8X4),
+                        lhsT_scale=x_sc[:, d, :],
+                        rhs=codes[:].bitcast(FP8X4),
+                        rhs_scale=scales[:],
+                        start=True,
+                        stop=True,
+                    )
+                banks.append(bank[:].rearrange("p d (m t) -> p d t m", t=PACK))
+            return banks
+
+        M = HALF // PACK
+        gate = [sb.tile([P, D, PACK, M], F32, name="gate%d" % h) for h in range(2)]
+        mix_b = sb.tile([P, D, PACK, M], F32, name="mix_b")
+        mix = [raw_1a[:].rearrange("p d (t m) -> p d t m", t=PACK), mix_b[:]]
+        terms = sb.tile([P, D, PACK, P], F32, name="terms")
+
+        def tanh(h, banks):
+            for e in range(2):
+                nc.scalar.activation(gate[h][:, 2 * e : 2 * e + 2], banks[e], ACT.Tanh)
+
+        def mix_vector(h, ds):
+            for d in ds:
+                nc.vector.tensor_scalar(
+                    mix[h][:, d], gate[h][:, d], 2.0, stat_vd[:, d : d + 1], ALU.add, ALU.mult
+                )
+
+        def mix_scalar(h, ds):
+            for d in ds:
+                nc.scalar.activation(
+                    mix[h][:, d], gate[h][:, d], ACT.Identity,
+                    bias=stat2_vd[:, d : d + 1], scale=stat_vd[:, d : d + 1],
+                )
+
+        def multiply(bank, ds, ts, m0, m1):
+            h = m0 // M
+            nc.vector.tensor_tensor(
+                terms[:, ds, ts, m0:m1],
+                bank[:, :, ts, :],
+                mix[h][:, ds, ts, m0 - h * M : m1 - h * M],
+                ALU.mult,
+            )
+
+        grp_ga = grouped_tile("grp_ga", HALF)
+        grp_gb = grouped_tile("grp_gb", HALF)
+        grp_1a = grouped_tile("grp_1a", 256)
+        grp_1b = grouped_tile("grp_1b", 128)
+        grp_1c = grouped_tile("grp_1c", 128)
+        grp_o = grouped_tile("grp_o", N)
+
+        cast(nc.scalar.copy, grp_ga, raw_ga, 0, HALF)
+        picked_scales = sb.tile([P, S], U8, name="picked_scales")
+        nc.vector.tensor_copy(picked_scales[:], scale_table[:].indirect(offsets[:]))
+        qga = quantize("ga", grp_ga, HALF)
+        x_sc = sb.tile([P, D, V], U8, name="x_sc", align_bytes=64)
+        nc.vector.tensor_copy(x_sc[:], picked_scales[:].rearrange("p (v d) -> p d v", d=D))
+        x_codes = sb.tile([P, D, V], U32, name="x_codes", align_bytes=64)
+        nc.vector.tensor_copy(
+            x_codes[:].rearrange("p d v -> p v d"), x_table[:].bitcast(U32).indirect(offsets[:])
+        )
+
+        ga = project("ga", ("b0", "b1"), qga, HALF)
+        cast(nc.scalar.copy, grp_gb, raw_gb, 0, 128)
+        cast(nc.vector.tensor_copy, grp_gb, raw_gb, 128, HALF)
+        tanh(0, ga)
+        qgb = quantize("gb", grp_gb, HALF)
+        gb = project("gb", ("b2", "b3"), qgb, HALF)
+        cast(nc.vector.tensor_copy, grp_1a, raw_1a, 0, 256)
+        tanh(1, gb)
+        cast(nc.vector.tensor_copy, grp_1b, raw_1b, 0, 128)
+        q1a = quantize("1a", grp_1a, 256)
+        ha = project("ha", ("b4", "b5"), q1a, 256)
+        cast(nc.vector.tensor_copy, grp_1c, raw_1c, 0, 128)
+        q1b = quantize("1b", grp_1b, 128)
+        hb = project("hb", ("b6",), q1b, 128)
+        mix_vector(0, (0, 1))
+        q1c = quantize("1c", grp_1c, 128)
+        hc = project("hc", ("b7",), q1c, 128)
+        mix_vector(0, (2, 3))
+        mix_scalar(1, range(D))
+
+        summed = ps.tile([P, PACK, V], F32, name="summed", tag="b0")
+        for u in range(2):
+            ts = slice(2 * u, 2 * u + 2)
+            multiply(ha[0], slice(0, 2), ts, 0, 64)
+            multiply(ha[1], slice(2, 4), ts, 0, 64)
+            multiply(hb[0], slice(0, 4), ts, 64, 96)
+            multiply(hc[0], slice(0, 4), ts, 96, 128)
+            for t in range(2 * u, 2 * u + 2):
+                for d in range(D):
+                    nc.tensor.matmul(
+                        summed[:, t, :], terms[:, d, t, :], ident[:],
+                        start=(d == 0), stop=(d == D - 1), is_transpose=True,
+                    )
+        cast(nc.vector.tensor_copy, grp_o, raw_o, 0, N)
+        o_codes, o_scales = quantize("o", grp_o, N)
+
+        mid = sb.tile([P, V, PACK], F32, name="mid")
+        grp_z = grouped_tile("grp_z", V)
+        HV = V // 2
+        for r in range(2):
+            vs = slice(r * HV, (r + 1) * HV)
+            nc.scalar.activation(mid[:, vs, :], summed[:].rearrange("p t v -> p v t")[:, vs, :], ACT.Silu, scale=0.5)
+            nc.vector.tensor_tensor(
+                grp_z[:, vs, :], mid[:, vs, :], unit_pt[:].unsqueeze(1).to_broadcast([P, HV, PACK]), ALU.mult
+            )
+        z_codes, z_scales = quantize("z", grp_z, V)
+
+        for r in range(2):
+            acc = ps.tile([P, V], F32, name="acc%d" % r, tag="b%d" % (2 + r))
+            cols = slice(r * P, (r + 1) * P)
+            nc.tensor.matmul_mx(
+                out=acc[:],
+                lhsT=o_codes[:, cols].bitcast(FP8X4),
+                lhsT_scale=o_scales[:, cols],
+                rhs=z_codes[:].bitcast(FP8X4),
+                rhs_scale=z_scales[:],
+                start=True,
+                stop=True,
+            )
+            res = sb.tile([P, V], F32, name="res%d" % r)
+            if r == 0:
+                nc.vector.tensor_copy(res[:], acc[:])
+                nc.sync.dma_start(out[cols, :], res[:])
+            else:
+                nc.scalar.copy(res[:], acc[:])
+                nc.scalar.dma_start(out[cols, :], res[:])

@@ -7,7 +7,6 @@ K, T, S, D, N, H = 512, 2048, 512, 4, 256, 512
 V = S // D
 P = 128
 PACK = 4
-HALF = H // 2
 FLOPS = 2 * (2 * K * H * S + H * N * V)
 
 F32 = mybir.dt.float32
@@ -29,58 +28,65 @@ def tile_picked_yhyper_in_p_kernel(
         sb = ctx.enter_context(tc.tile_pool(name="sb", bufs=1))
         ps = ctx.enter_context(tc.psum_pool(name="ps", bufs=1))
 
-        def load(name, w, c0, width):
-            raw = sb.tile([P, PACK, width], F32, name=name)
-            nc.sync.dma_start(raw[:], w.rearrange("(p j) c -> p j c", j=PACK)[:, :, c0 : c0 + width])
+        def tile(shape, dtype, name, tag=None):
+            return sb.tile(shape, dtype, name=name, tag=tag or name, align_bytes=64)[:]
+
+        def load(raw, w, c0):
+            width = raw.shape[2]
+            nc.sync.dma_start(raw, w.rearrange("(p j) c -> p j c", j=PACK)[:, :, c0 : c0 + width])
             return raw
 
-        scale_table = sb.tile([P, T], U8, name="scale_table")
-        nc.vector.memset(scale_table[:].bitcast(I32), 0)
-
+        scale_table = tile([P, T], U8, "scale_table")
+        nc.vector.memset(scale_table.bitcast(I32), 0)
+        raw_ga = load(tile([P, PACK, 256], F32, "raw_ga"), wg, 0)
         offsets = sb.tile([P, S // 16], U16, name="offsets")
         nc.sync.dma_start(offsets[:], offs)
-        raw_ga = load("raw_ga", wg, 0, HALF)
         for q in range(4):
             nc.sync.dma_start(
                 scale_table[32 * q : 32 * q + 4, :].bitcast(I32),
                 x_scales[0, 4 * q : 4 * q + 4, :].bitcast(I32),
             )
-        x_table = sb.tile([P, T], I32, name="x_table")
-        nc.sync.dma_start(x_table[:], x_words[0].rearrange("p n t -> p (n t)").bitcast(I32))
-        raw_gb = load("raw_gb", wg, HALF, HALF)
-        raw_1a = load("raw_1a", w1, 0, 256)
-        raw_1b = load("raw_1b", w1, 256, 128)
-        raw_1c = load("raw_1c", w1, 384, 128)
-        raw_o = load("raw_o", wo, 0, N)
+        x_table = tile([P, T], I32, "x_table")
+        nc.sync.dma_start(x_table, x_words[0].rearrange("p n t -> p (n t)").bitcast(I32))
+        stat_vd = tile([P, D], F32, "stat_vd")
+        nc.sync.dma_start(stat_vd, stat[0, :].rearrange("(v d) -> v d", d=D))
+        raw_gb = load(tile([P, PACK, 256], F32, "raw_gb"), wg, 256)
+        raw_1a = load(tile([P, PACK, 256], F32, "raw_1a"), w1, 0)
+        raw_1b = load(tile([P, PACK, 256], F32, "raw_1b"), w1, 256)
+        raw_o = load(tile([P, PACK, N], F32, "raw_o"), wo, 0)
+        unit_pt = tile([P, PACK], F32, "unit_pt")
+        nc.sync.dma_start(unit_pt, unit.rearrange("(p t) o -> p (t o)", t=PACK))
 
-        stat_vd = sb.tile([P, D], F32, name="stat_vd")
-        nc.gpsimd.dma_start(stat_vd[:], stat[0, :].rearrange("(v d) -> v d", d=D))
-        unit_pt = sb.tile([P, PACK], F32, name="unit_pt")
-        nc.gpsimd.dma_start(unit_pt[:], unit.rearrange("(p t) o -> p (t o)", t=PACK))
-        stat2_vd = sb.tile([P, D], F32, name="stat2_vd")
-        nc.gpsimd.tensor_scalar(stat2_vd[:], stat_vd[:], 2.0, 0.0, ALU.mult, ALU.add)
-        ident = sb.tile([P, P], F32, name="ident")
-        make_identity(nc, ident[:])
+        warm_in = tile([P, 1], F32, "warm_in")
+        warm_out = tile([P, 1], F32, "warm_out")
+        nc.vector.memset(warm_in, 0.0)
+        nc.scalar.activation(warm_out, warm_in, ACT.Silu)
+        ident = tile([P, P], F32, "ident")
+        make_identity(nc, ident)
 
-        def grouped_tile(name, width):
-            return sb.tile([P, width, PACK], BF16, name=name, align_bytes=64)
-
-        def cast(copy, dst, raw, c0, c1):
+        def cast_part(copy, grouped, raw, c0, c1):
             copy(
-                dst[:, c0:c1, :].rearrange("p (c i) t -> p c t i", i=4),
+                grouped[:, c0:c1].rearrange("p (c i) t -> p c t i", i=4),
                 raw[:, :, c0:c1].rearrange("p t (c i) -> p c t i", i=4),
             )
 
-        def quantize(name, grouped, width):
-            codes = sb.tile([P, width], U32, name=name + "_codes", align_bytes=64)
-            scales = sb.tile([P, width], U8, name=name + "_scales", align_bytes=64)
+        def cast(copy, name, raw, tag=None):
+            grouped = tile([P, raw.shape[2], PACK], BF16, name, tag)
+            cast_part(copy, grouped, raw, 0, raw.shape[2])
+            return grouped
+
+        def quantize(name, grouped, tag=None):
+            width = grouped.shape[1]
+            codes = tile([P, width], U32, name + "_codes", tag)
+            scales = tile([P, width], U8, name + "_scales")
             nc.vector.quantize_mx(
-                out=codes[:].bitcast(FP8X4), scales=scales[:], in_=grouped[:].rearrange("p c t -> p (c t)")
+                out=codes.bitcast(FP8X4), scales=scales, in_=grouped.rearrange("p c t -> p (c t)")
             )
             return codes, scales
 
-        def project(name, tags, w, width):
+        def project(name, tags, w):
             codes, scales = w
+            width = codes.shape[1]
             per_bank = 512 // width
             banks = []
             for e in range(D // per_bank):
@@ -91,110 +97,111 @@ def tile_picked_yhyper_in_p_kernel(
                         out=bank[:, dd, :],
                         lhsT=x_codes[:, d, :].bitcast(FP8X4),
                         lhsT_scale=x_sc[:, d, :],
-                        rhs=codes[:].bitcast(FP8X4),
-                        rhs_scale=scales[:],
+                        rhs=codes.bitcast(FP8X4),
+                        rhs_scale=scales,
                         start=True,
                         stop=True,
                     )
                 banks.append(bank[:].rearrange("p d (m t) -> p d t m", t=PACK))
             return banks
 
-        M = HALF // PACK
-        gate = [sb.tile([P, D, PACK, M], F32, name="gate%d" % h) for h in range(2)]
-        mix_b = sb.tile([P, D, PACK, M], F32, name="mix_b")
-        mix = [raw_1a[:].rearrange("p d (t m) -> p d t m", t=PACK), mix_b[:]]
-        terms = sb.tile([P, D, PACK, P], F32, name="terms")
+        def mix_vector(dst, gate, d):
+            nc.vector.tensor_scalar(dst, gate, 2.0, stat_vd[:, d : d + 1], ALU.add, ALU.mult)
 
-        def tanh(h, banks):
-            for e in range(2):
-                nc.scalar.activation(gate[h][:, 2 * e : 2 * e + 2], banks[e], ACT.Tanh)
-
-        def mix_vector(h, ds):
-            for d in ds:
-                nc.vector.tensor_scalar(
-                    mix[h][:, d], gate[h][:, d], 2.0, stat_vd[:, d : d + 1], ALU.add, ALU.mult
-                )
-
-        def mix_scalar(h, ds):
-            for d in ds:
-                nc.scalar.activation(
-                    mix[h][:, d], gate[h][:, d], ACT.Identity,
-                    bias=stat2_vd[:, d : d + 1], scale=stat_vd[:, d : d + 1],
-                )
-
-        def multiply(bank, ds, ts, m0, m1):
-            h = m0 // M
-            nc.vector.tensor_tensor(
-                terms[:, ds, ts, m0:m1],
-                bank[:, :, ts, :],
-                mix[h][:, ds, ts, m0 - h * M : m1 - h * M],
-                ALU.mult,
+        def mix_scalar(dst, gate, d):
+            nc.scalar.activation(
+                dst, gate, ACT.Identity, bias=stat2_vd[:, d : d + 1], scale=stat_vd[:, d : d + 1]
             )
 
-        grp_ga = grouped_tile("grp_ga", HALF)
-        grp_gb = grouped_tile("grp_gb", HALF)
-        grp_1a = grouped_tile("grp_1a", 256)
-        grp_1b = grouped_tile("grp_1b", 128)
-        grp_1c = grouped_tile("grp_1c", 128)
-        grp_o = grouped_tile("grp_o", N)
-
-        cast(nc.scalar.copy, grp_ga, raw_ga, 0, HALF)
-        picked_scales = sb.tile([P, S], U8, name="picked_scales")
-        nc.vector.tensor_copy(picked_scales[:], scale_table[:].indirect(offsets[:]))
-        qga = quantize("ga", grp_ga, HALF)
-        x_sc = sb.tile([P, D, V], U8, name="x_sc", align_bytes=64)
-        nc.vector.tensor_copy(x_sc[:], picked_scales[:].rearrange("p (v d) -> p d v", d=D))
-        x_codes = sb.tile([P, D, V], U32, name="x_codes", align_bytes=64)
+        grp_ga = cast(nc.scalar.copy, "grp_ga", raw_ga)
+        stat2_vd = tile([P, D], F32, "stat2_vd")
+        nc.scalar.mul(stat2_vd, stat_vd, 2.0)
+        picked_scales = tile([P, S], U8, "picked_scales")
+        nc.vector.tensor_copy(picked_scales, scale_table.indirect(offsets[:]))
+        qga = quantize("ga", grp_ga, "scale_table")
+        x_sc = tile([P, D, V], U8, "x_sc")
+        nc.vector.tensor_copy(x_sc, picked_scales.rearrange("p (v d) -> p d v", d=D))
+        x_codes = tile([P, D, V], U32, "x_codes")
         nc.vector.tensor_copy(
-            x_codes[:].rearrange("p d v -> p v d"), x_table[:].bitcast(U32).indirect(offsets[:])
+            x_codes.rearrange("p d v -> p v d"), x_table.bitcast(U32).indirect(offsets[:])
         )
 
-        ga = project("ga", ("b0", "b1"), qga, HALF)
-        cast(nc.scalar.copy, grp_gb, raw_gb, 0, 128)
-        cast(nc.vector.tensor_copy, grp_gb, raw_gb, 128, HALF)
-        tanh(0, ga)
-        qgb = quantize("gb", grp_gb, HALF)
-        gb = project("gb", ("b2", "b3"), qgb, HALF)
-        cast(nc.vector.tensor_copy, grp_1a, raw_1a, 0, 256)
-        tanh(1, gb)
-        cast(nc.vector.tensor_copy, grp_1b, raw_1b, 0, 128)
-        q1a = quantize("1a", grp_1a, 256)
-        ha = project("ha", ("b4", "b5"), q1a, 256)
-        cast(nc.vector.tensor_copy, grp_1c, raw_1c, 0, 128)
-        q1b = quantize("1b", grp_1b, 128)
-        hb = project("hb", ("b6",), q1b, 128)
-        mix_vector(0, (0, 1))
-        q1c = quantize("1c", grp_1c, 128)
-        hc = project("hc", ("b7",), q1c, 128)
-        mix_vector(0, (2, 3))
-        mix_scalar(1, range(D))
+        ga = project("ga", ("b0", "b1"), qga)
+        grp_gb = tile([P, 256, PACK], BF16, "grp_gb")
+        cast_part(nc.scalar.copy, grp_gb, raw_gb, 0, 192)
+        cast_part(nc.vector.tensor_copy, grp_gb, raw_gb, 192, 256)
+        gate_lo = tile([P, D, PACK, 64], F32, "gate_lo", "raw_gb")
+        for e in range(2):
+            nc.scalar.activation(gate_lo[:, 2 * e : 2 * e + 2], ga[e], ACT.Tanh)
+        qgb = quantize("gb", grp_gb)
+        gb = project("gb", ("b2", "b3"), qgb)
+        mix_lo01 = tile([P, 2, PACK, 64], F32, "mix_lo01")
+        for d in range(2):
+            mix_scalar(mix_lo01[:, d], gate_lo[:, d], d)
+        grp_1a = cast(nc.vector.tensor_copy, "grp_1a", raw_1a)
+        gate_hi = tile([P, D, PACK, 64], F32, "gate_hi")
+        for e in range(2):
+            nc.scalar.activation(gate_hi[:, 2 * e : 2 * e + 2], gb[e], ACT.Tanh)
+        grp_1b = tile([P, 256, PACK], BF16, "grp_1b")
+        cast_part(nc.vector.tensor_copy, grp_1b, raw_1b, 0, 128)
+        q1a = quantize("1a", grp_1a)
+        ha = project("ha", ("b4", "b5"), q1a)
+        cast_part(nc.vector.tensor_copy, grp_1b, raw_1b, 128, 256)
+        mix_lo23 = tile([P, 2, PACK, 64], F32, "mix_lo23", "grp_1a")
+        mix_vector(mix_lo23[:, 0], gate_lo[:, 2], 2)
+        q1b = quantize("1b", grp_1b)
+        hb = project("hb", ("b6", "b7"), q1b)
+        mix_vector(mix_lo23[:, 1], gate_lo[:, 3], 3)
+        warm_bank = ps.tile([P, S], F32, name="warm_bank", tag="b1")
+        for r in range(2):
+            nc.tensor.matmul_mx(
+                out=warm_bank[:],
+                lhsT=q1b[0][:, 0:P].bitcast(FP8X4),
+                lhsT_scale=q1b[1][:, 0:P],
+                rhs=x_codes.rearrange("p d v -> p (d v)").bitcast(FP8X4),
+                rhs_scale=x_sc.rearrange("p d v -> p (d v)"),
+                start=True,
+                stop=True,
+            )
+        mix_hi = [tile([P, D, 2, 64], F32, "mix_hi%d" % u) for u in range(2)]
+        for u in range(2):
+            for d in range(D):
+                mix_scalar(mix_hi[u][:, d], gate_hi[:, d, 2 * u : 2 * u + 2], d)
+        grp_o = cast(nc.scalar.copy, "grp_o", raw_o, "gate_hi")
 
         summed = ps.tile([P, PACK, V], F32, name="summed", tag="b0")
-        for u in range(2):
-            ts = slice(2 * u, 2 * u + 2)
-            multiply(ha[0], slice(0, 2), ts, 0, 64)
-            multiply(ha[1], slice(2, 4), ts, 0, 64)
-            multiply(hb[0], slice(0, 4), ts, 64, 96)
-            multiply(hc[0], slice(0, 4), ts, 96, 128)
-            for t in range(2 * u, 2 * u + 2):
-                for d in range(D):
-                    nc.tensor.matmul(
-                        summed[:, t, :], terms[:, d, t, :], ident[:],
-                        start=(d == 0), stop=(d == D - 1), is_transpose=True,
-                    )
-        cast(nc.vector.tensor_copy, grp_o, raw_o, 0, N)
-        o_codes, o_scales = quantize("o", grp_o, N)
+        terms = tile([P, D, PACK, P], F32, "terms")
 
-        mid = sb.tile([P, V, PACK], F32, name="mid")
-        grp_z = grouped_tile("grp_z", V)
+        def transposes(t):
+            for d in range(D):
+                nc.tensor.matmul(
+                    summed[:, t, :], terms[:, d, t, :], ident,
+                    start=(d == 0), stop=(d == D - 1), is_transpose=True,
+                )
+
+        nc.vector.tensor_tensor(terms[:, 0:2, :, 0:64], ha[0], mix_lo01, ALU.mult)
+        nc.vector.tensor_tensor(terms[:, 2:4, 0:2, 0:64], ha[1][:, :, 0:2], mix_lo23[:, :, 0:2], ALU.mult)
+        nc.vector.tensor_tensor(terms[:, 0:2, 0:2, 64:128], hb[0][:, :, 0:2], mix_hi[0][:, 0:2], ALU.mult)
+        nc.vector.tensor_tensor(terms[:, 2:4, 0:2, 64:128], hb[1][:, :, 0:2], mix_hi[0][:, 2:4], ALU.mult)
+        transposes(0)
+        transposes(1)
+        nc.vector.tensor_tensor(terms[:, 2:4, 2:4, 0:64], ha[1][:, :, 2:4], mix_lo23[:, :, 2:4], ALU.mult)
+        nc.vector.tensor_tensor(terms[:, 0:2, 2:4, 64:128], hb[0][:, :, 2:4], mix_hi[1][:, 0:2], ALU.mult)
+        for t in (2, 3):
+            nc.vector.tensor_tensor(terms[:, 2:4, t, 64:128], hb[1][:, :, t], mix_hi[1][:, 2:4, t - 2], ALU.mult)
+            transposes(t)
+        o_codes, o_scales = quantize("o", grp_o, "mix_hi1")
+
+        mid = tile([P, V, PACK], F32, "mid")
+        grp_z = tile([P, V, PACK], BF16, "grp_z")
         HV = V // 2
         for r in range(2):
             vs = slice(r * HV, (r + 1) * HV)
             nc.scalar.activation(mid[:, vs, :], summed[:].rearrange("p t v -> p v t")[:, vs, :], ACT.Silu, scale=0.5)
             nc.vector.tensor_tensor(
-                grp_z[:, vs, :], mid[:, vs, :], unit_pt[:].unsqueeze(1).to_broadcast([P, HV, PACK]), ALU.mult
+                grp_z[:, vs, :], mid[:, vs, :], unit_pt.unsqueeze(1).to_broadcast([P, HV, PACK]), ALU.mult
             )
-        z_codes, z_scales = quantize("z", grp_z, V)
+        z_codes, z_scales = quantize("z", grp_z)
 
         for r in range(2):
             acc = ps.tile([P, V], F32, name="acc%d" % r, tag="b%d" % (2 + r))
@@ -203,15 +210,15 @@ def tile_picked_yhyper_in_p_kernel(
                 out=acc[:],
                 lhsT=o_codes[:, cols].bitcast(FP8X4),
                 lhsT_scale=o_scales[:, cols],
-                rhs=z_codes[:].bitcast(FP8X4),
-                rhs_scale=z_scales[:],
+                rhs=z_codes.bitcast(FP8X4),
+                rhs_scale=z_scales,
                 start=True,
                 stop=True,
             )
-            res = sb.tile([P, V], F32, name="res%d" % r)
+            res = tile([P, V], F32, "res%d" % r)
             if r == 0:
-                nc.vector.tensor_copy(res[:], acc[:])
-                nc.sync.dma_start(out[cols, :], res[:])
+                nc.vector.tensor_copy(res, acc[:])
+                nc.sync.dma_start(out[cols, :], res)
             else:
-                nc.scalar.copy(res[:], acc[:])
-                nc.scalar.dma_start(out[cols, :], res[:])
+                nc.scalar.copy(res, acc[:])
+                nc.scalar.dma_start(out[cols, :], res)

@@ -142,69 +142,58 @@ def tile_picked_yhyper_in_p_kernel(
         gate_hi = tile([P, D, PACK, 64], F32, "gate_hi")
         for e in range(2):
             nc.scalar.activation(gate_hi[:, 2 * e : 2 * e + 2], gb[e], ACT.Tanh)
-        grp_1b = tile([P, 256, PACK], BF16, "grp_1b")
-        cast_part(nc.vector.tensor_copy, grp_1b, raw_1b, 0, 128)
         q1a = quantize("1a", grp_1a)
         ha = project("ha", ("b4", "b5"), q1a)
-        cast_part(nc.vector.tensor_copy, grp_1b, raw_1b, 128, 256)
+        grp_1b = cast(nc.vector.tensor_copy, "grp_1b", raw_1b)
         mix_lo23 = tile([P, 2, PACK, 64], F32, "mix_lo23", "grp_1a")
         mix_vector(mix_lo23[:, 0], gate_lo[:, 2], 2)
+        mix_vector(mix_lo23[:, 1], gate_lo[:, 3], 3)
         q1b = quantize("1b", grp_1b)
         hb = project("hb", ("b6", "b7"), q1b)
-        mix_vector(mix_lo23[:, 1], gate_lo[:, 3], 3)
-        warm_bank = ps.tile([P, S], F32, name="warm_bank", tag="b1")
-        for r in range(2):
-            nc.tensor.matmul_mx(
-                out=warm_bank[:],
-                lhsT=q1b[0][:, 0:P].bitcast(FP8X4),
-                lhsT_scale=q1b[1][:, 0:P],
-                rhs=x_codes.rearrange("p d v -> p (d v)").bitcast(FP8X4),
-                rhs_scale=x_sc.rearrange("p d v -> p (d v)"),
-                start=True,
-                stop=True,
-            )
         mix_hi = [tile([P, D, 2, 64], F32, "mix_hi%d" % u) for u in range(2)]
         for u in range(2):
             for d in range(D):
                 mix_scalar(mix_hi[u][:, d], gate_hi[:, d, 2 * u : 2 * u + 2], d)
-        grp_o = cast(nc.scalar.copy, "grp_o", raw_o, "gate_hi")
+        grp_o = tile([P, N, PACK], BF16, "grp_o", "grp_1b")
+        nc.gpsimd.tensor_scalar(grp_o, raw_o.rearrange("p t c -> p c t"), 1.0, 0.0, ALU.mult, ALU.add)
 
-        summed = ps.tile([P, PACK, V], F32, name="summed", tag="b0")
+        grp_z = tile([P, V, PACK], BF16, "grp_z")
         terms = tile([P, D, PACK, P], F32, "terms")
 
-        def transposes(t):
-            for d in range(D):
-                nc.tensor.matmul(
-                    summed[:, t, :], terms[:, d, t, :], ident,
-                    start=(d == 0), stop=(d == D - 1), is_transpose=True,
-                )
+        summed = [
+            ps.tile([P, V], F32, name="summed%d" % t, tag=("b0", "b2", "b3", "b1")[t]) for t in range(PACK)
+        ]
+
+        def transposes(ts, ds):
+            for t in ts:
+                for d in ds:
+                    nc.tensor.matmul(
+                        summed[t][:], terms[:, d, t, :], ident,
+                        start=(d == 0), stop=(d == D - 1), is_transpose=True,
+                    )
 
         nc.vector.tensor_tensor(terms[:, 0:2, :, 0:64], ha[0], mix_lo01, ALU.mult)
         nc.vector.tensor_tensor(terms[:, 2:4, 0:2, 0:64], ha[1][:, :, 0:2], mix_lo23[:, :, 0:2], ALU.mult)
         nc.vector.tensor_tensor(terms[:, 0:2, 0:2, 64:128], hb[0][:, :, 0:2], mix_hi[0][:, 0:2], ALU.mult)
+        transposes((0, 1), (0, 1))
         nc.vector.tensor_tensor(terms[:, 2:4, 0:2, 64:128], hb[1][:, :, 0:2], mix_hi[0][:, 2:4], ALU.mult)
-        transposes(0)
-        transposes(1)
-        nc.vector.tensor_tensor(terms[:, 2:4, 2:4, 0:64], ha[1][:, :, 2:4], mix_lo23[:, :, 2:4], ALU.mult)
+        transposes((0, 1), (2, 3))
         nc.vector.tensor_tensor(terms[:, 0:2, 2:4, 64:128], hb[0][:, :, 2:4], mix_hi[1][:, 0:2], ALU.mult)
+        transposes((2, 3), (0, 1))
+        nc.vector.tensor_tensor(terms[:, 2:4, 2:4, 0:64], ha[1][:, :, 2:4], mix_lo23[:, :, 2:4], ALU.mult)
         for t in (2, 3):
             nc.vector.tensor_tensor(terms[:, 2:4, t, 64:128], hb[1][:, :, t], mix_hi[1][:, 2:4, t - 2], ALU.mult)
-            transposes(t)
+            transposes((t,), (2, 3))
         o_codes, o_scales = quantize("o", grp_o, "mix_hi1")
 
-        mid = tile([P, V, PACK], F32, "mid")
-        grp_z = tile([P, V, PACK], BF16, "grp_z")
-        HV = V // 2
-        for r in range(2):
-            vs = slice(r * HV, (r + 1) * HV)
-            nc.scalar.activation(mid[:, vs, :], summed[:].rearrange("p t v -> p v t")[:, vs, :], ACT.Silu, scale=0.5)
-            nc.vector.tensor_tensor(
-                grp_z[:, vs, :], mid[:, vs, :], unit_pt.unsqueeze(1).to_broadcast([P, HV, PACK]), ALU.mult
-            )
+        for t in range(PACK):
+            mid = tile([P, V], F32, "mid%d" % t)
+            nc.scalar.activation(mid, summed[t][:], ACT.Silu, scale=0.5)
+            nc.vector.tensor_scalar(grp_z[:, :, t], mid, unit_pt[:, t : t + 1], None, ALU.mult)
         z_codes, z_scales = quantize("z", grp_z)
 
         for r in range(2):
-            acc = ps.tile([P, V], F32, name="acc%d" % r, tag="b%d" % (2 + r))
+            acc = ps.tile([P, V], F32, name="acc%d" % r, tag="b%d" % (4 + r))
             cols = slice(r * P, (r + 1) * P)
             nc.tensor.matmul_mx(
                 out=acc[:],

@@ -150,6 +150,17 @@ def tile_picked_yhyper_in_p_kernel(
         mix_vector(mix_lo23[:, 1], gate_lo[:, 3], 3)
         q1b = quantize("1b", grp_1b)
         hb = project("hb", ("b6", "b7"), q1b)
+        warm_bank = ps.tile([P, S], F32, name="warm_bank", tag="b1")
+        for r in range(2):
+            nc.tensor.matmul_mx(
+                out=warm_bank[:],
+                lhsT=q1b[0][:, 0:P].bitcast(FP8X4),
+                lhsT_scale=q1b[1][:, 0:P],
+                rhs=x_codes.rearrange("p d v -> p (d v)").bitcast(FP8X4),
+                rhs_scale=x_sc.rearrange("p d v -> p (d v)"),
+                start=True,
+                stop=True,
+            )
         mix_hi = [tile([P, D, 2, 64], F32, "mix_hi%d" % u) for u in range(2)]
         for u in range(2):
             for d in range(D):

from contextlib import ExitStack

import concourse.mybir as mybir
from concourse.masks import make_identity

K, T, S, D, N, H = 512, 2048, 512, 4, 256, 512
V = S // D
P = 128
PACK = 4
FLOPS = 2 * (2 * K * H * S + H * N * V)

F32 = mybir.dt.float32
BF16 = mybir.dt.bfloat16
I32 = mybir.dt.int32
U32 = mybir.dt.uint32
U16 = mybir.dt.uint16
U8 = mybir.dt.uint8
FP8X4 = mybir.dt.float8_e4m3fn_x4
ACT = mybir.ActivationFunctionType
ALU = mybir.AluOpType


def tile_picked_yhyper_in_p_kernel(
    tc, x_words, x_scales, w1, wg, stat, unit, wo, offs, out
):
    nc = tc.nc
    with ExitStack() as ctx:
        sb = ctx.enter_context(tc.tile_pool(name="sb", bufs=1))
        ps = ctx.enter_context(tc.psum_pool(name="ps", bufs=1))

        def tile(shape, dtype, name, tag=None):
            return sb.tile(shape, dtype, name=name, tag=tag or name, align_bytes=64)[:]

        def load(raw, w, c0):
            width = raw.shape[2]
            nc.sync.dma_start(raw, w.rearrange("(p j) c -> p j c", j=PACK)[:, :, c0 : c0 + width])
            return raw

        scale_table = tile([P, T], U8, "scale_table")
        nc.vector.memset(scale_table.bitcast(I32), 0)
        raw_ga = load(tile([P, PACK, 256], F32, "raw_ga"), wg, 0)
        offsets = sb.tile([P, S // 16], U16, name="offsets")
        nc.sync.dma_start(offsets[:], offs)
        for q in range(4):
            nc.sync.dma_start(
                scale_table[32 * q : 32 * q + 4, :].bitcast(I32),
                x_scales[0, 4 * q : 4 * q + 4, :].bitcast(I32),
            )
        x_table = tile([P, T], I32, "x_table")
        nc.sync.dma_start(x_table, x_words[0].rearrange("p n t -> p (n t)").bitcast(I32))
        stat_vd = tile([P, D], F32, "stat_vd")
        nc.sync.dma_start(stat_vd, stat[0, :].rearrange("(v d) -> v d", d=D))
        raw_gb = load(tile([P, PACK, 256], F32, "raw_gb"), wg, 256)
        raw_1a = load(tile([P, PACK, 256], F32, "raw_1a"), w1, 0)
        raw_1b = load(tile([P, PACK, 256], F32, "raw_1b"), w1, 256)
        raw_o = load(tile([P, PACK, N], F32, "raw_o"), wo, 0)
        unit_pt = tile([P, PACK], F32, "unit_pt")
        nc.sync.dma_start(unit_pt, unit.rearrange("(p t) o -> p (t o)", t=PACK))

        warm_in = tile([P, 1], F32, "warm_in")
        warm_out = tile([P, 1], F32, "warm_out")
        nc.vector.memset(warm_in, 0.0)
        nc.scalar.activation(warm_out, warm_in, ACT.Silu)
        ident = tile([P, P], F32, "ident")
        make_identity(nc, ident)

        def cast_part(copy, grouped, raw, c0, c1):
            copy(
                grouped[:, c0:c1].rearrange("p (c i) t -> p c t i", i=4),
                raw[:, :, c0:c1].rearrange("p t (c i) -> p c t i", i=4),
            )

        def cast(copy, name, raw, tag=None):
            grouped = tile([P, raw.shape[2], PACK], BF16, name, tag)
            cast_part(copy, grouped, raw, 0, raw.shape[2])
            return grouped

        def quantize(name, grouped, tag=None):
            width = grouped.shape[1]
            codes = tile([P, width], U32, name + "_codes", tag)
            scales = tile([P, width], U8, name + "_scales")
            nc.vector.quantize_mx(
                out=codes.bitcast(FP8X4), scales=scales, in_=grouped.rearrange("p c t -> p (c t)")
            )
            return codes, scales

        def project(name, tags, w):
            codes, scales = w
            width = codes.shape[1]
            per_bank = 512 // width
            banks = []
            for e in range(D // per_bank):
                bank = ps.tile([P, per_bank, width], F32, name=name + str(e), tag=tags[e])
                for dd in range(per_bank):
                    d = per_bank * e + dd
                    nc.tensor.matmul_mx(
                        out=bank[:, dd, :],
                        lhsT=x_codes[:, d, :].bitcast(FP8X4),
                        lhsT_scale=x_sc[:, d, :],
                        rhs=codes.bitcast(FP8X4),
                        rhs_scale=scales,
                        start=True,
                        stop=True,
                    )
                banks.append(bank[:].rearrange("p d (m t) -> p d t m", t=PACK))
            return banks

        def mix_vector(dst, gate, d):
            nc.vector.tensor_scalar(dst, gate, 2.0, stat_vd[:, d : d + 1], ALU.add, ALU.mult)

        def mix_scalar(dst, gate, d):
            nc.scalar.activation(
                dst, gate, ACT.Identity, bias=stat2_vd[:, d : d + 1], scale=stat_vd[:, d : d + 1]
            )

        grp_ga = cast(nc.scalar.copy, "grp_ga", raw_ga)
        stat2_vd = tile([P, D], F32, "stat2_vd")
        nc.scalar.mul(stat2_vd, stat_vd, 2.0)
        picked_scales = tile([P, S], U8, "picked_scales")
        nc.vector.tensor_copy(picked_scales, scale_table.indirect(offsets[:]))
        qga = quantize("ga", grp_ga, "scale_table")
        x_sc = tile([P, D, V], U8, "x_sc")
        nc.vector.tensor_copy(x_sc, picked_scales.rearrange("p (v d) -> p d v", d=D))
        x_codes = tile([P, D, V], U32, "x_codes")
        nc.vector.tensor_copy(
            x_codes.rearrange("p d v -> p v d"), x_table.bitcast(U32).indirect(offsets[:])
        )

        ga = project("ga", ("b0", "b1"), qga)
        grp_gb = tile([P, 256, PACK], BF16, "grp_gb")
        cast_part(nc.scalar.copy, grp_gb, raw_gb, 0, 192)
        cast_part(nc.vector.tensor_copy, grp_gb, raw_gb, 192, 256)
        gate_lo = tile([P, D, PACK, 64], F32, "gate_lo", "raw_gb")
        for e in range(2):
            nc.scalar.activation(gate_lo[:, 2 * e : 2 * e + 2], ga[e], ACT.Tanh)
        qgb = quantize("gb", grp_gb)
        gb = project("gb", ("b2", "b3"), qgb)
        mix_lo01 = tile([P, 2, PACK, 64], F32, "mix_lo01")
        for d in range(2):
            mix_scalar(mix_lo01[:, d], gate_lo[:, d], d)
        grp_1a = cast(nc.vector.tensor_copy, "grp_1a", raw_1a)
        gate_hi = tile([P, D, PACK, 64], F32, "gate_hi")
        for e in range(2):
            nc.scalar.activation(gate_hi[:, 2 * e : 2 * e + 2], gb[e], ACT.Tanh)
        q1a = quantize("1a", grp_1a)
        ha = project("ha", ("b4", "b5"), q1a)
        grp_1b = cast(nc.vector.tensor_copy, "grp_1b", raw_1b)
        mix_lo23 = tile([P, 2, PACK, 64], F32, "mix_lo23", "grp_1a")
        mix_vector(mix_lo23[:, 0], gate_lo[:, 2], 2)
        mix_vector(mix_lo23[:, 1], gate_lo[:, 3], 3)
        q1b = quantize("1b", grp_1b)
        hb = project("hb", ("b6", "b7"), q1b)
        warm_bank = ps.tile([P, S], F32, name="warm_bank", tag="b1")
        for r in range(2):
            nc.tensor.matmul_mx(
                out=warm_bank[:],
                lhsT=q1b[0][:, 0:P].bitcast(FP8X4),
                lhsT_scale=q1b[1][:, 0:P],
                rhs=x_codes.rearrange("p d v -> p (d v)").bitcast(FP8X4),
                rhs_scale=x_sc.rearrange("p d v -> p (d v)"),
                start=True,
                stop=True,
            )
        mix_hi = [tile([P, D, 2, 64], F32, "mix_hi%d" % u) for u in range(2)]
        for u in range(2):
            for d in range(D):
                mix_scalar(mix_hi[u][:, d], gate_hi[:, d, 2 * u : 2 * u + 2], d)
        grp_o = tile([P, N, PACK], BF16, "grp_o", "grp_1b")
        nc.gpsimd.tensor_scalar(grp_o, raw_o.rearrange("p t c -> p c t"), 1.0, 0.0, ALU.mult, ALU.add)

        grp_z = tile([P, V, PACK], BF16, "grp_z")
        terms = tile([P, D, PACK, P], F32, "terms")

        summed = [
            ps.tile([P, V], F32, name="summed%d" % t, tag=("b0", "b2", "b3", "b1")[t]) for t in range(PACK)
        ]

        def transposes(ts, ds):
            for t in ts:
                for d in ds:
                    nc.tensor.matmul(
                        summed[t][:], terms[:, d, t, :], ident,
                        start=(d == 0), stop=(d == D - 1), is_transpose=True,
                    )

        nc.vector.tensor_tensor(terms[:, 0:2, :, 0:64], ha[0], mix_lo01, ALU.mult)
        nc.vector.tensor_tensor(terms[:, 2:4, 0:2, 0:64], ha[1][:, :, 0:2], mix_lo23[:, :, 0:2], ALU.mult)
        nc.vector.tensor_tensor(terms[:, 0:2, 0:2, 64:128], hb[0][:, :, 0:2], mix_hi[0][:, 0:2], ALU.mult)
        transposes((0, 1), (0, 1))
        nc.vector.tensor_tensor(terms[:, 2:4, 0:2, 64:128], hb[1][:, :, 0:2], mix_hi[0][:, 2:4], ALU.mult)
        transposes((0, 1), (2, 3))
        nc.vector.tensor_tensor(terms[:, 0:2, 2:4, 64:128], hb[0][:, :, 2:4], mix_hi[1][:, 0:2], ALU.mult)
        transposes((2, 3), (0, 1))
        nc.vector.tensor_tensor(terms[:, 2:4, 2:4, 0:64], ha[1][:, :, 2:4], mix_lo23[:, :, 2:4], ALU.mult)
        for t in (2, 3):
            nc.vector.tensor_tensor(terms[:, 2:4, t, 64:128], hb[1][:, :, t], mix_hi[1][:, 2:4, t - 2], ALU.mult)
            transposes((t,), (2, 3))
        o_codes, o_scales = quantize("o", grp_o, "mix_hi1")

        for t in range(PACK):
            mid = tile([P, V], F32, "mid%d" % t)
            nc.scalar.activation(mid, summed[t][:], ACT.Silu, scale=0.5)
            nc.vector.tensor_scalar(grp_z[:, :, t], mid, unit_pt[:, t : t + 1], None, ALU.mult)
        z_codes, z_scales = quantize("z", grp_z)

        for r in range(2):
            acc = ps.tile([P, V], F32, name="acc%d" % r, tag="b%d" % (4 + r))
            cols = slice(r * P, (r + 1) * P)
            nc.tensor.matmul_mx(
                out=acc[:],
                lhsT=o_codes[:, cols].bitcast(FP8X4),
                lhsT_scale=o_scales[:, cols],
                rhs=z_codes.bitcast(FP8X4),
                rhs_scale=z_scales,
                start=True,
                stop=True,
            )
            res = tile([P, V], F32, "res%d" % r)
            if r == 0:
                nc.vector.tensor_copy(res, acc[:])
                nc.sync.dma_start(out[cols, :], res)
            else:
                nc.scalar.copy(res, acc[:])
                nc.scalar.dma_start(out[cols, :], res)
